import numpy as np
import ml_dtypes


def mxq(x, axis, fmt="e4m3"):
    dtype, down = {"e4m3": (ml_dtypes.float8_e4m3fn, 7), "e5m2": (ml_dtypes.float8_e5m2, 14)}[fmt]
    v = np.moveaxis(np.asarray(x, np.float32).astype(ml_dtypes.bfloat16).astype(np.float64), axis, -1)
    blocks = v.reshape(v.shape[:-1] + (-1, 32))
    amax = np.abs(blocks).max(-1, keepdims=True)
    byte = np.maximum(np.where(amax > 0, np.frexp(amax)[1] - 1 + 127, 0) - down, 1)
    scale = np.exp2(byte - 127.0)
    codes = (blocks / scale).astype(np.float32).astype(dtype).astype(np.float64)
    return np.moveaxis((codes * scale).reshape(v.shape), -1, axis)


WIDE = False


def mx_kscale(k):
    if not WIDE:
        return np.ones(k)
    levels = np.array([10, -10, 5, -5, 0])
    if k % 512:
        return np.exp2(np.random.permutation(np.resize(levels, k // 32))).repeat(32)
    a = np.empty((k // 512, 16))
    for p in range(k // 512):
        a[p, :8] = np.random.permutation(np.resize(levels, 8))
        for g in range(8):
            far = levels[np.abs(levels - a[p, g]) >= 10]
            a[p, g + 8] = far[np.random.randint(len(far))]
    return np.exp2(a.ravel()).repeat(32)


def f64(x):
    return np.asarray(x).astype(np.float64)


def striped(idx):
    return np.tile(idx.reshape(-1, 16).T, (8, 1)).astype(np.uint16)


def unstriped(offs):
    return offs[:16].T.reshape(-1).astype(np.int64)


def pack_weight(w):
    k, n = w.shape
    w = f64(np.asarray(w, np.float32).astype(ml_dtypes.bfloat16)).reshape(k // 32, 32, n)
    amax = np.abs(w).max(1)
    byte = np.clip(np.where(amax > 0, np.frexp(amax)[1] - 1 + 127 - 7, 1), 1, 254)
    scaled = (w * np.exp2(127.0 - byte)[:, None, :]).reshape(k, n).astype(np.float32)
    words = np.ascontiguousarray(scaled.reshape(k // 512, 128, 4, n).transpose(0, 1, 3, 2)).astype(ml_dtypes.float8_e4m3fn).view(np.uint8)
    return words, np.ascontiguousarray(byte.astype(np.uint8).reshape(k // 512, 16, n))


def unpack_weight(words, scales):
    g, p, n, _ = words.shape
    vals = np.ascontiguousarray(words).view(ml_dtypes.float8_e4m3fn).astype(np.float64) * np.repeat(np.exp2(scales.astype(np.float64) - 127.0), 8, axis=1)[..., None]
    return vals.transpose(0, 1, 3, 2).reshape(g * 512, n)


K, T, S, H, N, W = 512, 2048, 512, 512, 128, 2048
P = 2 ** 7


def setup_inputs():
    n = np.random.standard_normal
    s = mx_kscale(K)[:, None]
    u = mx_kscale(H)
    packed_xT = pack_weight(n((K, T)) * s)
    packed_eT = pack_weight(n((K, W)) * s)
    return {
        "x_words": packed_xT[0],
        "x_scales": packed_xT[1],
        "w1": (n((K, H)) / np.sqrt(K) / s).astype(np.float32),
        "e_words": packed_eT[0],
        "e_scales": packed_eT[1],
        "cond": (np.tile(np.random.uniform(0.7, 1.3, S), (P, 1))).astype(np.float32),
        "across": (np.random.uniform(0.2, 0.9, (H, 1))).astype(np.float32),
        "within": (np.random.uniform(0.05, 0.4, (H, 1))).astype(np.float32),
        "unit": (np.random.uniform(0.5, 1.5, (H, 1)) * u[:, None]).astype(np.float32),
        "wo": (n((H, N)) / np.sqrt(H) / u[:, None]).astype(np.float32),
        "offs": striped(np.random.permutation(T)[:S]),
        "test": striped(np.random.permutation(W)[:S]),
    }


def reference(x_words, x_scales, w1, e_words, e_scales, cond, across, within, unit, wo, offs, test):
    xq = unpack_weight(x_words, x_scales)[:, unstriped(offs)]
    w1q = mxq(f64(w1), 0, "e4m3")
    pa = w1q.T @ xq
    e_test = unpack_weight(e_words, e_scales)[:, unstriped(test)]
    pb = w1q.T @ e_test
    pc = pb * f64(cond)[:1]
    qd = f64(across) * (pa * pc) - (0.5 * (f64(within) * ((pa) ** 2 + (pc) ** 2)))
    nn = np.sqrt((pa) ** 2 + (pc) ** 2 + 0.3)
    qn = qd / nn
    zz = f64(unit) * qn
    return np.tanh(mxq(f64(wo), 0, "e4m3").T @ mxq(zz, 0, "e4m3"))

@@ -1,0 +1,179 @@
+from contextlib import ExitStack
+
+import concourse.mybir as mybir
+
+F32 = mybir.dt.float32
+BF16 = mybir.dt.bfloat16
+I32 = mybir.dt.int32
+U32 = mybir.dt.uint32
+U16 = mybir.dt.uint16
+U8 = mybir.dt.uint8
+FP8X4 = mybir.dt.float8_e4m3fn_x4
+ACT = mybir.ActivationFunctionType
+ALU = mybir.AluOpType
+
+P = 128
+PACK = 4
+K, T, S, H, N = 512, 2048, 512, 512, 128
+HALF = S // 2
+FLOPS = 2 * K * H * S * 2 + 2 * H * N * S
+
+
+def tile_picked_yplda_len_p_kernel(tc, x_words, x_scales, w1, e_words, e_scales, cond, across, within, unit, wo, offs, test, out):
+    nc = tc.nc
+    with ExitStack() as ctx:
+        keep = ctx.enter_context(tc.tile_pool(name="keep", bufs=1))
+        psum = ctx.enter_context(tc.psum_pool(name="psum", bufs=1))
+
+        def sb(name, shape, dtype):
+            return keep.tile(shape, dtype, name=name, align_bytes=64)
+
+        test_list = keep.tile([P, S // 16], U16, name="test_list")
+        offs_list = keep.tile([P, S // 16], U16, name="offs_list")
+        e_scale_table = sb("e_scale_table", [P, T], U8)
+        x_scale_table = sb("x_scale_table", [P, T], U8)
+        nc.vector.memset(e_scale_table[:].bitcast(I32), 0)
+        nc.vector.memset(x_scale_table[:].bitcast(I32), 0)
+        warm = sb("warm", [P, 2], F32)
+        nc.vector.memset(warm[:, 0:1], 1.0)
+        nc.scalar.activation(out=warm[:, 1:2], in_=warm[:, 0:1], func=ACT.Abs_reciprocal_sqrt)
+
+        def load_scales(table, scales):
+            for q in range(4):
+                nc.sync.dma_start(out=table[32 * q : 32 * q + 4, :].bitcast(I32), in_=scales[0, 4 * q : 4 * q + 4, :].bitcast(I32))
+
+        def load_words(name, words):
+            table = sb(name, [P, T], I32)
+            nc.sync.dma_start(out=table[:], in_=words[0].rearrange("p n t -> p (n t)").bitcast(I32))
+            return table
+
+        nc.sync.dma_start(test_list[:], test)
+        load_scales(e_scale_table, e_scales)
+        nc.sync.dma_start(offs_list[:], offs)
+        w1_rows = w1.rearrange("(p j) c -> p j c", j=PACK)
+        w1_raw = []
+        for h in range(2):
+            raw = sb("w1_raw%d" % h, [P, PACK, H // 2], F32)
+            nc.sync.dma_start(out=raw[:], in_=w1_rows[:, :, h * (H // 2) : (h + 1) * (H // 2)])
+            w1_raw.append(raw)
+        e_word_table = load_words("e_word_table", e_words)
+        load_scales(x_scale_table, x_scales)
+        cond_sb = sb("cond_sb", [P, S], F32)
+        nc.sync.dma_start(out=cond_sb[:], in_=cond)
+        cols = {}
+        for name, vec in (("across", across), ("within", within), ("unit", unit)):
+            cols[name] = sb(name + "_sb", [P, PACK], F32)
+            nc.sync.dma_start(out=cols[name][:], in_=vec.rearrange("(p t) o -> p (t o)", t=PACK))
+        x_word_table = load_words("x_word_table", x_words)
+        wo_raw = sb("wo_raw", [P, PACK, N], F32)
+        nc.sync.dma_start(out=wo_raw[:], in_=wo.rearrange("(p j) n -> p j n", j=PACK))
+
+        e_scale = sb("e_scale", [P, S], U8)
+        x_scale = sb("x_scale", [P, S], U8)
+        nc.vector.tensor_copy(e_scale[:], e_scale_table[:].indirect(test_list[:]))
+        nc.vector.tensor_copy(x_scale[:], x_scale_table[:].indirect(offs_list[:]))
+
+        w1_bf = sb("w1_bf", [P, PACK, P, PACK], BF16)
+        for h in range(2):
+            nc.scalar.copy(
+                out=w1_bf[:, :, 64 * h : 64 * h + 64, :].rearrange("p t m j -> p m t j"),
+                in_=w1_raw[h][:].rearrange("p j (m t) -> p m t j", t=PACK),
+            )
+        w1_code = sb("w1_code", [P, H], U32)
+        w1_scale = sb("w1_scale", [P, H], U8)
+        nc.vector.quantize_mx(out=w1_code[:].bitcast(FP8X4), scales=w1_scale[:], in_=w1_bf[:].rearrange("p t m j -> p (t m j)"))
+
+        def project(side, h, word_table, lst, scale):
+            code = sb("%s_code%d" % (side, h), [P, HALF], U32)
+            nc.vector.tensor_copy(code[:], word_table[:].bitcast(U32).indirect(lst[:, 16 * h : 16 * h + 16]))
+            banks = []
+            for b in range(2):
+                bank = psum.tile([P, 2, HALF], F32, name="%s_bank%d%d" % (side, h, b), tag="%s%d%d" % (side, h, b))
+                for u in range(2):
+                    t = 2 * b + u
+                    nc.tensor.matmul_mx(
+                        out=bank[:, u, :],
+                        lhsT=w1_code[:, t * P : (t + 1) * P].bitcast(FP8X4),
+                        lhsT_scale=w1_scale[:, t * P : (t + 1) * P],
+                        rhs=code[:].bitcast(FP8X4),
+                        rhs_scale=scale[:, h * HALF : (h + 1) * HALF],
+                        start=True,
+                        stop=True,
+                    )
+                banks.append(bank)
+            return banks
+
+        pc, c2 = [], []
+        for h in range(2):
+            banks = project("e", h, e_word_table, test_list, e_scale)
+            pc.append(sb("pc%d" % h, [P, PACK, HALF], F32))
+            c2.append(sb("c2%d" % h, [P, PACK, HALF], F32))
+            for b in range(2):
+                nc.vector.tensor_tensor(
+                    out=pc[h][:, 2 * b : 2 * b + 2, :],
+                    in0=banks[b][:],
+                    in1=cond_sb[:, h * HALF : (h + 1) * HALF].unsqueeze(1).to_broadcast([P, 2, HALF]),
+                    op=ALU.mult,
+                )
+                nc.scalar.activation(out=c2[h][:, 2 * b : 2 * b + 2, :], in_=pc[h][:, 2 * b : 2 * b + 2, :], func=ACT.Square)
+
+        cross_w = sb("cross_w", [P, PACK], F32)
+        square_w = sb("square_w", [P, PACK], F32)
+        nc.vector.tensor_tensor(out=cross_w[:], in0=cols["across"][:], in1=cols["unit"][:], op=ALU.mult)
+        nc.vector.scalar_tensor_tensor(out=square_w[:], in0=cols["within"][:], scalar=-0.5, in1=cols["unit"][:], op0=ALU.mult, op1=ALU.mult)
+
+        wo_bf = sb("wo_bf", [P, N, PACK], BF16)
+        nc.scalar.copy(
+            out=wo_bf[:].rearrange("p (c i) j -> p c j i", i=4),
+            in_=wo_raw[:].rearrange("p j (c i) -> p c j i", i=4),
+        )
+        wo_code = sb("wo_code", [P, N], U32)
+        wo_scale = sb("wo_scale", [P, N], U8)
+        nc.vector.quantize_mx(out=wo_code[:].bitcast(FP8X4), scales=wo_scale[:], in_=wo_bf[:].rearrange("p n j -> p (n j)"))
+
+        xbanks = [project("x", h, x_word_table, offs_list, x_scale) for h in range(2)]
+        sums, scores = [], []
+        for h in range(2):
+            a2 = sb("a2%d" % h, [P, PACK, HALF], F32)
+            cross = sb("cross%d" % h, [P, PACK, HALF], F32)
+            ssum = sb("ssum%d" % h, [P, PACK, HALF], F32)
+            rinv = sb("rinv%d" % h, [P, PACK, HALF], F32)
+            qd = sb("qd%d" % h, [P, PACK, HALF], F32)
+            sums.append(ssum)
+            for b in range(2):
+                pair = slice(2 * b, 2 * b + 2)
+                nc.scalar.activation(out=a2[:, pair, :], in_=xbanks[h][b][:], func=ACT.Square)
+                for u in range(2):
+                    t = 2 * b + u
+                    nc.vector.scalar_tensor_tensor(out=cross[:, t, :], in0=xbanks[h][b][:, u, :], scalar=cross_w[:, t : t + 1], in1=pc[h][:, t, :], op0=ALU.mult, op1=ALU.mult)
+            for b in range(2):
+                pair = slice(2 * b, 2 * b + 2)
+                nc.vector.tensor_tensor(out=ssum[:, pair, :], in0=a2[:, pair, :], in1=c2[h][:, pair, :], op=ALU.add)
+                nc.scalar.activation(out=rinv[:, pair, :], in_=ssum[:, pair, :], func=ACT.Abs_reciprocal_sqrt, bias=0.3)
+            for t in range(PACK):
+                nc.vector.scalar_tensor_tensor(out=qd[:, t, :], in0=ssum[:, t, :], scalar=square_w[:, t : t + 1], in1=cross[:, t, :], op0=ALU.mult, op1=ALU.add)
+            zz = sb("zz%d" % h, [P, HALF, PACK], BF16)
+            nc.vector.tensor_tensor(
+                out=zz[:].rearrange("p (c i) t -> p c t i", i=4),
+                in0=qd[:].rearrange("p t (c i) -> p c t i", i=4),
+                in1=rinv[:].rearrange("p t (c i) -> p c t i", i=4),
+                op=ALU.mult,
+            )
+            zz_code = sb("zz_code%d" % h, [P, HALF], U32)
+            zz_scale = sb("zz_scale%d" % h, [P, HALF], U8)
+            nc.vector.quantize_mx(out=zz_code[:].bitcast(FP8X4), scales=zz_scale[:], in_=zz[:].rearrange("p c t -> p (c t)"))
+            score = psum.tile([P, HALF], F32, name="score%d" % h, tag="e%d0" % h)
+            nc.tensor.matmul_mx(
+                out=score[:],
+                lhsT=wo_code[:].bitcast(FP8X4),
+                lhsT_scale=wo_scale[:],
+                rhs=zz_code[:].bitcast(FP8X4),
+                rhs_scale=zz_scale[:],
+                start=True,
+                stop=True,
+            )
+            scores.append(score)
+        for h in range(2):
+            res = sums[1][:, 2 + h, :]
+            nc.scalar.activation(out=res, in_=scores[h][:], func=ACT.Tanh)
+            nc.sync.dma_start(out=out[:, h * HALF : (h + 1) * HALF], in_=res)

@@ -1,6 +1,7 @@
 from contextlib import ExitStack
 
 import concourse.mybir as mybir
+from concourse.masks import make_identity
 
 F32 = mybir.dt.float32
 BF16 = mybir.dt.bfloat16
@@ -16,6 +17,8 @@ P = 128
 PACK = 4
 K, T, S, H, N = 512, 2048, 512, 512, 128
 HALF = S // 2
+CHUNKS = S // P
+PC_ON_VECTOR = 2
 FLOPS = 2 * K * H * S * 2 + 2 * H * N * S
 
 
@@ -28,15 +31,20 @@ def tile_picked_yplda_len_p_kernel(tc, x_words, x_scales, w1, e_words, e_scales,
         def sb(name, shape, dtype):
             return keep.tile(shape, dtype, name=name, align_bytes=64)
 
+        def dealt(bank):
+            return bank[:].rearrange("p (m t) -> p t m", t=PACK)
+
         test_list = keep.tile([P, S // 16], U16, name="test_list")
         offs_list = keep.tile([P, S // 16], U16, name="offs_list")
         e_scale_table = sb("e_scale_table", [P, T], U8)
         x_scale_table = sb("x_scale_table", [P, T], U8)
-        nc.vector.memset(e_scale_table[:].bitcast(I32), 0)
+        nc.gpsimd.memset(e_scale_table[:].bitcast(I32), 0)
         nc.vector.memset(x_scale_table[:].bitcast(I32), 0)
         warm = sb("warm", [P, 2], F32)
         nc.vector.memset(warm[:, 0:1], 1.0)
         nc.scalar.activation(out=warm[:, 1:2], in_=warm[:, 0:1], func=ACT.Abs_reciprocal_sqrt)
+        ident = sb("ident", [P, P], F32)
+        make_identity(nc, ident[:])
 
         def load_scales(table, scales):
             for q in range(4):
@@ -49,7 +57,6 @@ def tile_picked_yplda_len_p_kernel(tc, x_words, x_scales, w1, e_words, e_scales,
 
         nc.sync.dma_start(test_list[:], test)
         load_scales(e_scale_table, e_scales)
-        nc.sync.dma_start(offs_list[:], offs)
         w1_rows = w1.rearrange("(p j) c -> p j c", j=PACK)
         w1_raw = []
         for h in range(2):
@@ -57,73 +64,78 @@ def tile_picked_yplda_len_p_kernel(tc, x_words, x_scales, w1, e_words, e_scales,
             nc.sync.dma_start(out=raw[:], in_=w1_rows[:, :, h * (H // 2) : (h + 1) * (H // 2)])
             w1_raw.append(raw)
         e_word_table = load_words("e_word_table", e_words)
+        nc.sync.dma_start(offs_list[:], offs)
         load_scales(x_scale_table, x_scales)
-        cond_sb = sb("cond_sb", [P, S], F32)
-        nc.sync.dma_start(out=cond_sb[:], in_=cond)
+        cond_col = sb("cond_col", [P, CHUNKS], F32)
+        with nc.allow_non_contiguous_dma(reason="one factor a partition and chunk"):
+            nc.sync.dma_start(out=cond_col[:], in_=cond[0].rearrange("(g p) -> p g", p=P))
+        x_word_table = load_words("x_word_table", x_words)
         cols = {}
         for name, vec in (("across", across), ("within", within), ("unit", unit)):
             cols[name] = sb(name + "_sb", [P, PACK], F32)
             nc.sync.dma_start(out=cols[name][:], in_=vec.rearrange("(p t) o -> p (t o)", t=PACK))
-        x_word_table = load_words("x_word_table", x_words)
         wo_raw = sb("wo_raw", [P, PACK, N], F32)
         nc.sync.dma_start(out=wo_raw[:], in_=wo.rearrange("(p j) n -> p j n", j=PACK))
 
         e_scale = sb("e_scale", [P, S], U8)
         x_scale = sb("x_scale", [P, S], U8)
         nc.vector.tensor_copy(e_scale[:], e_scale_table[:].indirect(test_list[:]))
-        nc.vector.tensor_copy(x_scale[:], x_scale_table[:].indirect(offs_list[:]))
 
-        w1_bf = sb("w1_bf", [P, PACK, P, PACK], BF16)
-        for h in range(2):
-            nc.scalar.copy(
-                out=w1_bf[:, :, 64 * h : 64 * h + 64, :].rearrange("p t m j -> p m t j"),
-                in_=w1_raw[h][:].rearrange("p j (m t) -> p m t j", t=PACK),
-            )
         w1_code = sb("w1_code", [P, H], U32)
         w1_scale = sb("w1_scale", [P, H], U8)
-        nc.vector.quantize_mx(out=w1_code[:].bitcast(FP8X4), scales=w1_scale[:], in_=w1_bf[:].rearrange("p t m j -> p (t m j)"))
+        for h in range(2):
+            w1_bf = sb("w1_bf%d" % h, [P, H // 2, PACK], BF16)
+            nc.scalar.copy(
+                out=w1_bf[:].rearrange("p (c i) j -> p c j i", i=4),
+                in_=w1_raw[h][:].rearrange("p j (c i) -> p c j i", i=4),
+            )
+            part = slice(h * (H // 2), (h + 1) * (H // 2))
+            nc.vector.quantize_mx(out=w1_code[:, part].bitcast(FP8X4), scales=w1_scale[:, part], in_=w1_bf[:].rearrange("p c j -> p (c j)"))
 
-        def project(side, h, word_table, lst, scale):
-            code = sb("%s_code%d" % (side, h), [P, HALF], U32)
-            nc.vector.tensor_copy(code[:], word_table[:].bitcast(U32).indirect(lst[:, 16 * h : 16 * h + 16]))
+        def project(side, word_table, lst, scale):
             banks = []
-            for b in range(2):
-                bank = psum.tile([P, 2, HALF], F32, name="%s_bank%d%d" % (side, h, b), tag="%s%d%d" % (side, h, b))
+            for h in range(2):
+                code = sb("%s_code%d" % (side, h), [P, HALF], U32)
+                nc.vector.tensor_copy(code[:], word_table[:].bitcast(U32).indirect(lst[:, 16 * h : 16 * h + 16]))
                 for u in range(2):
-                    t = 2 * b + u
+                    g = 2 * h + u
+                    bank = psum.tile([P, H], F32, name="%s_bank%d" % (side, g), tag="%s%d" % (side, g))
                     nc.tensor.matmul_mx(
-                        out=bank[:, u, :],
-                        lhsT=w1_code[:, t * P : (t + 1) * P].bitcast(FP8X4),
-                        lhsT_scale=w1_scale[:, t * P : (t + 1) * P],
-                        rhs=code[:].bitcast(FP8X4),
-                        rhs_scale=scale[:, h * HALF : (h + 1) * HALF],
+                        out=bank[:],
+                        lhsT=code[:, u * P : (u + 1) * P].bitcast(FP8X4),
+                        lhsT_scale=scale[:, g * P : (g + 1) * P],
+                        rhs=w1_code[:].bitcast(FP8X4),
+                        rhs_scale=w1_scale[:],
                         start=True,
                         stop=True,
                     )
-                banks.append(bank)
+                    banks.append(bank)
             return banks
 
-        pc, c2 = [], []
-        for h in range(2):
-            banks = project("e", h, e_word_table, test_list, e_scale)
-            pc.append(sb("pc%d" % h, [P, PACK, HALF], F32))
-            c2.append(sb("c2%d" % h, [P, PACK, HALF], F32))
-            for b in range(2):
-                nc.vector.tensor_tensor(
-                    out=pc[h][:, 2 * b : 2 * b + 2, :],
-                    in0=banks[b][:],
-                    in1=cond_sb[:, h * HALF : (h + 1) * HALF].unsqueeze(1).to_broadcast([P, 2, HALF]),
-                    op=ALU.mult,
-                )
-                nc.scalar.activation(out=c2[h][:, 2 * b : 2 * b + 2, :], in_=pc[h][:, 2 * b : 2 * b + 2, :], func=ACT.Square)
+        ebanks = project("e", e_word_table, test_list, e_scale)
+        nc.vector.tensor_copy(x_scale[:], x_scale_table[:].indirect(offs_list[:]))
+        pc, sums = [], []
+        for g in range(CHUNKS):
+            pc.append(sb("pc%d" % g, [P, PACK, P], F32))
+            c2 = sb("c2%d" % g, [P, PACK, P], F32)
+            factor = cond_col[:, g : g + 1]
+            if g < PC_ON_VECTOR:
+                nc.vector.tensor_scalar(out=pc[g][:], in0=dealt(ebanks[g]), scalar1=factor, scalar2=None, op0=ALU.mult)
+            else:
+                nc.scalar.activation(out=pc[g][:], in_=dealt(ebanks[g]), func=ACT.Copy, scale=factor)
+            nc.scalar.activation(out=c2[:], in_=dealt(ebanks[g]), func=ACT.Square, scale=factor)
+            sums.append(psum.tile([P, PACK, P], F32, name="sum%d" % g, tag="e%d" % g))
+            for t in range(PACK):
+                nc.tensor.matmul(out=sums[g][:, t, :], lhsT=c2[:, t, :], rhs=ident[:], is_transpose=True, start=(t == 0), stop=False)
+
+        xbanks = project("x", x_word_table, offs_list, x_scale)
 
         cross_w = sb("cross_w", [P, PACK], F32)
         square_w = sb("square_w", [P, PACK], F32)
         nc.vector.tensor_tensor(out=cross_w[:], in0=cols["across"][:], in1=cols["unit"][:], op=ALU.mult)
         nc.vector.scalar_tensor_tensor(out=square_w[:], in0=cols["within"][:], scalar=-0.5, in1=cols["unit"][:], op0=ALU.mult, op1=ALU.mult)
-
         wo_bf = sb("wo_bf", [P, N, PACK], BF16)
-        nc.scalar.copy(
+        nc.vector.tensor_copy(
             out=wo_bf[:].rearrange("p (c i) j -> p c j i", i=4),
             in_=wo_raw[:].rearrange("p j (c i) -> p c j i", i=4),
         )
@@ -131,38 +143,39 @@ def tile_picked_yplda_len_p_kernel(tc, x_words, x_scales, w1, e_words, e_scales,
         wo_scale = sb("wo_scale", [P, N], U8)
         nc.vector.quantize_mx(out=wo_code[:].bitcast(FP8X4), scales=wo_scale[:], in_=wo_bf[:].rearrange("p n j -> p (n j)"))
 
-        xbanks = [project("x", h, x_word_table, offs_list, x_scale) for h in range(2)]
-        sums, scores = [], []
-        for h in range(2):
-            a2 = sb("a2%d" % h, [P, PACK, HALF], F32)
-            cross = sb("cross%d" % h, [P, PACK, HALF], F32)
-            ssum = sb("ssum%d" % h, [P, PACK, HALF], F32)
-            rinv = sb("rinv%d" % h, [P, PACK, HALF], F32)
-            qd = sb("qd%d" % h, [P, PACK, HALF], F32)
-            sums.append(ssum)
-            for b in range(2):
-                pair = slice(2 * b, 2 * b + 2)
-                nc.scalar.activation(out=a2[:, pair, :], in_=xbanks[h][b][:], func=ACT.Square)
-                for u in range(2):
-                    t = 2 * b + u
-                    nc.vector.scalar_tensor_tensor(out=cross[:, t, :], in0=xbanks[h][b][:, u, :], scalar=cross_w[:, t : t + 1], in1=pc[h][:, t, :], op0=ALU.mult, op1=ALU.mult)
-            for b in range(2):
-                pair = slice(2 * b, 2 * b + 2)
-                nc.vector.tensor_tensor(out=ssum[:, pair, :], in0=a2[:, pair, :], in1=c2[h][:, pair, :], op=ALU.add)
-                nc.scalar.activation(out=rinv[:, pair, :], in_=ssum[:, pair, :], func=ACT.Abs_reciprocal_sqrt, bias=0.3)
+        crosses = []
+        for g in range(CHUNKS):
+            a2 = sb("a2%d" % g, [P, PACK, P], F32)
+            nc.scalar.activation(out=a2[:], in_=dealt(xbanks[g]), func=ACT.Square)
             for t in range(PACK):
-                nc.vector.scalar_tensor_tensor(out=qd[:, t, :], in0=ssum[:, t, :], scalar=square_w[:, t : t + 1], in1=cross[:, t, :], op0=ALU.mult, op1=ALU.add)
-            zz = sb("zz%d" % h, [P, HALF, PACK], BF16)
+                nc.tensor.matmul(out=sums[g][:, t, :], lhsT=a2[:, t, :], rhs=ident[:], is_transpose=True, start=False, stop=(t == PACK - 1))
+            prod = sb("prod%d" % g, [P, PACK, P], F32)
+            nc.vector.tensor_tensor(out=prod[:], in0=dealt(xbanks[g]), in1=pc[g][:], op=ALU.mult)
+            crosses.append(psum.tile([P, PACK, P], F32, name="cross%d" % g, tag="x%d" % g))
+            for t in range(PACK):
+                nc.tensor.transpose(out=crosses[g][:, t, :], in_=prod[:, t, :], identity=ident[:])
+
+        scores, weighted = [], []
+        for g in range(CHUNKS):
+            rinv = sb("rinv%d" % g, [P, PACK, P], F32)
+            weighted.append(sb("weighted%d" % g, [P, PACK, P], F32))
+            qd = sb("qd%d" % g, [P, PACK, P], F32)
+            nc.scalar.activation(out=rinv[:], in_=sums[g][:], func=ACT.Abs_reciprocal_sqrt, bias=0.3)
+            for t in range(PACK):
+                nc.scalar.activation(out=weighted[g][:, t, :], in_=sums[g][:, t, :], func=ACT.Copy, scale=square_w[:, t : t + 1])
+            for t in range(PACK):
+                nc.vector.scalar_tensor_tensor(out=qd[:, t, :], in0=crosses[g][:, t, :], scalar=cross_w[:, t : t + 1], in1=weighted[g][:, t, :], op0=ALU.mult, op1=ALU.add)
+            zz = sb("zz%d" % g, [P, P, PACK], BF16)
             nc.vector.tensor_tensor(
                 out=zz[:].rearrange("p (c i) t -> p c t i", i=4),
                 in0=qd[:].rearrange("p t (c i) -> p c t i", i=4),
                 in1=rinv[:].rearrange("p t (c i) -> p c t i", i=4),
                 op=ALU.mult,
             )
-            zz_code = sb("zz_code%d" % h, [P, HALF], U32)
-            zz_scale = sb("zz_scale%d" % h, [P, HALF], U8)
+            zz_code = sb("zz_code%d" % g, [P, P], U32)
+            zz_scale = sb("zz_scale%d" % g, [P, P], U8)
             nc.vector.quantize_mx(out=zz_code[:].bitcast(FP8X4), scales=zz_scale[:], in_=zz[:].rearrange("p c t -> p (c t)"))
-            score = psum.tile([P, HALF], F32, name="score%d" % h, tag="e%d0" % h)
+            score = psum.tile([P, P], F32, name="score%d" % g, tag="e%d" % g)
             nc.tensor.matmul_mx(
                 out=score[:],
                 lhsT=wo_code[:].bitcast(FP8X4),
@@ -173,7 +186,7 @@ def tile_picked_yplda_len_p_kernel(tc, x_words, x_scales, w1, e_words, e_scales,
                 stop=True,
             )
             scores.append(score)
-        for h in range(2):
-            res = sums[1][:, 2 + h, :]
-            nc.scalar.activation(out=res, in_=scores[h][:], func=ACT.Tanh)
-            nc.sync.dma_start(out=out[:, h * HALF : (h + 1) * HALF], in_=res)
+        for g in range(CHUNKS):
+            res = weighted[CHUNKS - 1][:, g, :]
+            nc.scalar.activation(out=res, in_=scores[g][:], func=ACT.Tanh)
+            nc.sync.dma_start(out=out[:, g * P : (g + 1) * P], in_=res)

@@ -18,7 +18,7 @@ PACK = 4
 K, T, S, H, N = 512, 2048, 512, 512, 128
 HALF = S // 2
 CHUNKS = S // P
-PC_ON_VECTOR = 2
+PC_ON_SCALAR = 2
 FLOPS = 2 * K * H * S * 2 + 2 * H * N * S
 
 
@@ -28,16 +28,21 @@ def tile_picked_yplda_len_p_kernel(tc, x_words, x_scales, w1, e_words, e_scales,
         keep = ctx.enter_context(tc.tile_pool(name="keep", bufs=1))
         psum = ctx.enter_context(tc.psum_pool(name="psum", bufs=1))
 
-        def sb(name, shape, dtype):
-            return keep.tile(shape, dtype, name=name, align_bytes=64)
+        def sb(name, shape, dtype, slot=None):
+            return keep.tile(shape, dtype, name=name, tag=slot or name, align_bytes=64)
 
         def dealt(bank):
             return bank[:].rearrange("p (m t) -> p t m", t=PACK)
+
+        def woven(tile_out, tile_in):
+            return tile_out.rearrange("p (c i) j -> p c j i", i=4), tile_in.rearrange("p j (c i) -> p c j i", i=4)
 
         test_list = keep.tile([P, S // 16], U16, name="test_list")
         offs_list = keep.tile([P, S // 16], U16, name="offs_list")
         e_scale_table = sb("e_scale_table", [P, T], U8)
         x_scale_table = sb("x_scale_table", [P, T], U8)
+        cond_rows = sb("cond_rows", [P, P], F32)
+        nc.vector.memset(cond_rows[:], 0.0)
         nc.gpsimd.memset(e_scale_table[:].bitcast(I32), 0)
         nc.vector.memset(x_scale_table[:].bitcast(I32), 0)
         warm = sb("warm", [P, 2], F32)
@@ -55,7 +60,13 @@ def tile_picked_yplda_len_p_kernel(tc, x_words, x_scales, w1, e_words, e_scales,
             nc.sync.dma_start(out=table[:], in_=words[0].rearrange("p n t -> p (n t)").bitcast(I32))
             return table
 
+        def load_column(name, vec):
+            col = sb(name, [P, PACK], F32)
+            nc.sync.dma_start(out=col[:], in_=vec.rearrange("(p t) o -> p (t o)", t=PACK))
+            return col
+
         nc.sync.dma_start(test_list[:], test)
+        nc.sync.dma_start(out=cond_rows[0:CHUNKS, :], in_=cond[0].rearrange("(g p) -> g p", p=P))
         load_scales(e_scale_table, e_scales)
         w1_rows = w1.rearrange("(p j) c -> p j c", j=PACK)
         w1_raw = []
@@ -66,30 +77,28 @@ def tile_picked_yplda_len_p_kernel(tc, x_words, x_scales, w1, e_words, e_scales,
         e_word_table = load_words("e_word_table", e_words)
         nc.sync.dma_start(offs_list[:], offs)
         load_scales(x_scale_table, x_scales)
-        cond_col = sb("cond_col", [P, CHUNKS], F32)
-        with nc.allow_non_contiguous_dma(reason="one factor a partition and chunk"):
-            nc.sync.dma_start(out=cond_col[:], in_=cond[0].rearrange("(g p) -> p g", p=P))
         x_word_table = load_words("x_word_table", x_words)
-        cols = {}
-        for name, vec in (("across", across), ("within", within), ("unit", unit)):
-            cols[name] = sb(name + "_sb", [P, PACK], F32)
-            nc.sync.dma_start(out=cols[name][:], in_=vec.rearrange("(p t) o -> p (t o)", t=PACK))
+        across_col = load_column("across_col", across)
+        within_col = load_column("within_col", within)
+        unit_col = load_column("unit_col", unit)
         wo_raw = sb("wo_raw", [P, PACK, N], F32)
         nc.sync.dma_start(out=wo_raw[:], in_=wo.rearrange("(p j) n -> p j n", j=PACK))
 
+        cond_turned = psum.tile([P, P], F32, name="cond_turned", tag="x3")
+        nc.tensor.transpose(out=cond_turned[:], in_=cond_rows[:], identity=ident[:])
+        cond_col = sb("cond_col", [P, CHUNKS], F32)
+        nc.scalar.copy(out=cond_col[:], in_=cond_turned[:, 0:CHUNKS])
+
         e_scale = sb("e_scale", [P, S], U8)
-        x_scale = sb("x_scale", [P, S], U8)
         nc.vector.tensor_copy(e_scale[:], e_scale_table[:].indirect(test_list[:]))
 
         w1_code = sb("w1_code", [P, H], U32)
         w1_scale = sb("w1_scale", [P, H], U8)
         for h in range(2):
-            w1_bf = sb("w1_bf%d" % h, [P, H // 2, PACK], BF16)
-            nc.scalar.copy(
-                out=w1_bf[:].rearrange("p (c i) j -> p c j i", i=4),
-                in_=w1_raw[h][:].rearrange("p j (c i) -> p c j i", i=4),
-            )
             part = slice(h * (H // 2), (h + 1) * (H // 2))
+            w1_bf = sb("w1_bf%d" % h, [P, H // 2, PACK], BF16)
+            dst, src = woven(w1_bf[:], w1_raw[h][:])
+            nc.scalar.copy(out=dst, in_=src)
             nc.vector.quantize_mx(out=w1_code[:, part].bitcast(FP8X4), scales=w1_scale[:, part], in_=w1_bf[:].rearrange("p c j -> p (c j)"))
 
         def project(side, word_table, lst, scale):
@@ -113,71 +122,87 @@ def tile_picked_yplda_len_p_kernel(tc, x_words, x_scales, w1, e_words, e_scales,
             return banks
 
         ebanks = project("e", e_word_table, test_list, e_scale)
+        x_scale = sb("x_scale", [P, S], U8, slot="e_word_table")
         nc.vector.tensor_copy(x_scale[:], x_scale_table[:].indirect(offs_list[:]))
-        pc, sums = [], []
-        for g in range(CHUNKS):
-            pc.append(sb("pc%d" % g, [P, PACK, P], F32))
-            c2 = sb("c2%d" % g, [P, PACK, P], F32)
-            factor = cond_col[:, g : g + 1]
-            if g < PC_ON_VECTOR:
-                nc.vector.tensor_scalar(out=pc[g][:], in0=dealt(ebanks[g]), scalar1=factor, scalar2=None, op0=ALU.mult)
-            else:
-                nc.scalar.activation(out=pc[g][:], in_=dealt(ebanks[g]), func=ACT.Copy, scale=factor)
-            nc.scalar.activation(out=c2[:], in_=dealt(ebanks[g]), func=ACT.Square, scale=factor)
-            sums.append(psum.tile([P, PACK, P], F32, name="sum%d" % g, tag="e%d" % g))
-            for t in range(PACK):
-                nc.tensor.matmul(out=sums[g][:, t, :], lhsT=c2[:, t, :], rhs=ident[:], is_transpose=True, start=(t == 0), stop=False)
-
         xbanks = project("x", x_word_table, offs_list, x_scale)
 
-        cross_w = sb("cross_w", [P, PACK], F32)
-        square_w = sb("square_w", [P, PACK], F32)
-        nc.vector.tensor_tensor(out=cross_w[:], in0=cols["across"][:], in1=cols["unit"][:], op=ALU.mult)
-        nc.vector.scalar_tensor_tensor(out=square_w[:], in0=cols["within"][:], scalar=-0.5, in1=cols["unit"][:], op0=ALU.mult, op1=ALU.mult)
-        wo_bf = sb("wo_bf", [P, N, PACK], BF16)
-        nc.vector.tensor_copy(
-            out=wo_bf[:].rearrange("p (c i) j -> p c j i", i=4),
-            in_=wo_raw[:].rearrange("p j (c i) -> p c j i", i=4),
-        )
+        late = sb("late", [P, T], F32, slot="x_word_table")
+        cross_w = late[:, 0:PACK]
+        square_w = late[:, PACK : 2 * PACK]
+        wo_bf = late[:, 16 : 16 + N * PACK // 2].bitcast(BF16)
         wo_code = sb("wo_code", [P, N], U32)
         wo_scale = sb("wo_scale", [P, N], U8)
-        nc.vector.quantize_mx(out=wo_code[:].bitcast(FP8X4), scales=wo_scale[:], in_=wo_bf[:].rearrange("p n j -> p (n j)"))
+        pc, sums, crosses, weighted, rinv, qd, zz = {}, {}, {}, {}, {}, {}, {}
 
-        crosses = []
-        for g in range(CHUNKS):
+        c2 = {}
+
+        def test_scaled(g):
+            if g == 0:
+                pc[g] = sb("pc0", [P, H], F32)[:].rearrange("p (t m) -> p t m", t=PACK)
+            else:
+                pc[g] = late[:, g * H : (g + 1) * H].rearrange("p (t m) -> p t m", t=PACK)
+            factor = cond_col[:, g : g + 1]
+            if g < PC_ON_SCALAR:
+                nc.scalar.activation(out=pc[g], in_=dealt(ebanks[g]), func=ACT.Copy, scale=factor)
+            else:
+                nc.vector.tensor_scalar(out=pc[g], in0=dealt(ebanks[g]), scalar1=factor, scalar2=None, op0=ALU.mult)
+
+        def test_square(g):
+            c2[g] = sb("c2%d" % g, [P, PACK, P], F32)
+            nc.scalar.activation(out=c2[g][:], in_=dealt(ebanks[g]), func=ACT.Square, scale=cond_col[:, g : g + 1])
+
+        def turn_test(g):
+            sums[g] = psum.tile([P, PACK, P], F32, name="sum%d" % g, tag="e%d" % g)
+            for t in range(PACK):
+                nc.tensor.matmul(out=sums[g][:, t, :], lhsT=c2[g][:, t, :], rhs=ident[:], is_transpose=True, start=(t == 0), stop=False)
+
+        def enrol_square(g):
             a2 = sb("a2%d" % g, [P, PACK, P], F32)
             nc.scalar.activation(out=a2[:], in_=dealt(xbanks[g]), func=ACT.Square)
             for t in range(PACK):
                 nc.tensor.matmul(out=sums[g][:, t, :], lhsT=a2[:, t, :], rhs=ident[:], is_transpose=True, start=False, stop=(t == PACK - 1))
+
+        def enrol_product(g):
             prod = sb("prod%d" % g, [P, PACK, P], F32)
-            nc.vector.tensor_tensor(out=prod[:], in0=dealt(xbanks[g]), in1=pc[g][:], op=ALU.mult)
-            crosses.append(psum.tile([P, PACK, P], F32, name="cross%d" % g, tag="x%d" % g))
+            nc.vector.tensor_tensor(out=prod[:], in0=dealt(xbanks[g]), in1=pc[g], op=ALU.mult)
+            crosses[g] = psum.tile([P, PACK, P], F32, name="cross%d" % g, tag="x%d" % g)
             for t in range(PACK):
                 nc.tensor.transpose(out=crosses[g][:, t, :], in_=prod[:, t, :], identity=ident[:])
 
-        scores, weighted = [], []
-        for g in range(CHUNKS):
-            rinv = sb("rinv%d" % g, [P, PACK, P], F32)
-            weighted.append(sb("weighted%d" % g, [P, PACK, P], F32))
-            qd = sb("qd%d" % g, [P, PACK, P], F32)
-            nc.scalar.activation(out=rinv[:], in_=sums[g][:], func=ACT.Abs_reciprocal_sqrt, bias=0.3)
+        def small_operands():
+            nc.vector.tensor_tensor(out=cross_w, in0=across_col[:], in1=unit_col[:], op=ALU.mult)
+            nc.vector.scalar_tensor_tensor(out=square_w, in0=within_col[:], scalar=-0.5, in1=unit_col[:], op0=ALU.mult, op1=ALU.mult)
+            dst, src = woven(wo_bf.rearrange("p (n j) -> p n j", j=PACK), wo_raw[:])
+            nc.vector.tensor_copy(out=dst, in_=src)
+            nc.vector.quantize_mx(out=wo_code[:].bitcast(FP8X4), scales=wo_scale[:], in_=wo_bf)
+
+        def combine(g):
+            weighted[g] = sb("weighted%d" % g, [P, PACK, P], F32)
+            rinv[g] = sb("rinv%d" % g, [P, PACK, P], F32)
+            qd[g] = sb("qd%d" % g, [P, PACK, P], F32)
+            root_first = g == CHUNKS - 1
+            if root_first:
+                nc.scalar.activation(out=rinv[g][:], in_=sums[g][:], func=ACT.Abs_reciprocal_sqrt, bias=0.3)
             for t in range(PACK):
                 nc.scalar.activation(out=weighted[g][:, t, :], in_=sums[g][:, t, :], func=ACT.Copy, scale=square_w[:, t : t + 1])
+            if not root_first:
+                nc.scalar.activation(out=rinv[g][:], in_=sums[g][:], func=ACT.Abs_reciprocal_sqrt, bias=0.3)
             for t in range(PACK):
-                nc.vector.scalar_tensor_tensor(out=qd[:, t, :], in0=crosses[g][:, t, :], scalar=cross_w[:, t : t + 1], in1=weighted[g][:, t, :], op0=ALU.mult, op1=ALU.add)
+                nc.vector.scalar_tensor_tensor(out=qd[g][:, t, :], in0=crosses[g][:, t, :], scalar=cross_w[:, t : t + 1], in1=weighted[g][:, t, :], op0=ALU.mult, op1=ALU.add)
+
+        def score(g, target):
             zz = sb("zz%d" % g, [P, P, PACK], BF16)
             nc.vector.tensor_tensor(
                 out=zz[:].rearrange("p (c i) t -> p c t i", i=4),
-                in0=qd[:].rearrange("p t (c i) -> p c t i", i=4),
-                in1=rinv[:].rearrange("p t (c i) -> p c t i", i=4),
+                in0=qd[g][:].rearrange("p t (c i) -> p c t i", i=4),
+                in1=rinv[g][:].rearrange("p t (c i) -> p c t i", i=4),
                 op=ALU.mult,
             )
             zz_code = sb("zz_code%d" % g, [P, P], U32)
             zz_scale = sb("zz_scale%d" % g, [P, P], U8)
             nc.vector.quantize_mx(out=zz_code[:].bitcast(FP8X4), scales=zz_scale[:], in_=zz[:].rearrange("p c t -> p (c t)"))
-            score = psum.tile([P, P], F32, name="score%d" % g, tag="e%d" % g)
             nc.tensor.matmul_mx(
-                out=score[:],
+                out=target,
                 lhsT=wo_code[:].bitcast(FP8X4),
                 lhsT_scale=wo_scale[:],
                 rhs=zz_code[:].bitcast(FP8X4),
@@ -185,8 +210,33 @@ def tile_picked_yplda_len_p_kernel(tc, x_words, x_scales, w1, e_words, e_scales,
                 start=True,
                 stop=True,
             )
-            scores.append(score)
+
+        last = CHUNKS - 1
+        test_scaled(0)
+        test_square(0)
+        turn_test(0)
+        test_square(1)
+        enrol_square(0)
+        test_scaled(1)
+        turn_test(1)
+        enrol_product(0)
+        small_operands()
+        scores = []
         for g in range(CHUNKS):
-            res = weighted[CHUNKS - 1][:, g, :]
-            nc.scalar.activation(out=res, in_=scores[g][:], func=ACT.Tanh)
-            nc.sync.dma_start(out=out[:, g * P : (g + 1) * P], in_=res)
+            if g + 2 < CHUNKS:
+                test_scaled(g + 2)
+            if g + 1 < CHUNKS:
+                enrol_square(g + 1)
+                enrol_product(g + 1)
+            if g + 2 < CHUNKS:
+                test_square(g + 2)
+                turn_test(g + 2)
+            combine(g)
+            scores.append(psum.tile([P, P], F32, name="scores%d" % g, tag="e%d" % g))
+            score(g, scores[g][:])
+        res = weighted[last]
+        for g in range(CHUNKS):
+            nc.scalar.activation(out=res[:, g, :], in_=scores[g][:], func=ACT.Tanh)
+            if g >= last - 1:
+                first = 0 if g < last else last
+                nc.sync.dma_start(out=out[:, first * P : (g + 1) * P], in_=res[:, first : g + 1, :].rearrange("p g c -> p (g c)"))

@@ -66,14 +66,14 @@ def tile_picked_yplda_len_p_kernel(tc, x_words, x_scales, w1, e_words, e_scales,
             return col
 
         nc.sync.dma_start(test_list[:], test)
-        nc.sync.dma_start(out=cond_rows[0:CHUNKS, :], in_=cond[0].rearrange("(g p) -> g p", p=P))
-        load_scales(e_scale_table, e_scales)
         w1_rows = w1.rearrange("(p j) c -> p j c", j=PACK)
         w1_raw = []
         for h in range(2):
             raw = sb("w1_raw%d" % h, [P, PACK, H // 2], F32)
             nc.sync.dma_start(out=raw[:], in_=w1_rows[:, :, h * (H // 2) : (h + 1) * (H // 2)])
             w1_raw.append(raw)
+        nc.sync.dma_start(out=cond_rows[0:CHUNKS, :], in_=cond[0].rearrange("(g p) -> g p", p=P))
+        load_scales(e_scale_table, e_scales)
         e_word_table = load_words("e_word_table", e_words)
         nc.sync.dma_start(offs_list[:], offs)
         load_scales(x_scale_table, x_scales)
@@ -87,10 +87,11 @@ def tile_picked_yplda_len_p_kernel(tc, x_words, x_scales, w1, e_words, e_scales,
         cond_turned = psum.tile([P, P], F32, name="cond_turned", tag="x3")
         nc.tensor.transpose(out=cond_turned[:], in_=cond_rows[:], identity=ident[:])
         cond_col = sb("cond_col", [P, CHUNKS], F32)
-        nc.scalar.copy(out=cond_col[:], in_=cond_turned[:, 0:CHUNKS])
 
         e_scale = sb("e_scale", [P, S], U8)
         nc.vector.tensor_copy(e_scale[:], e_scale_table[:].indirect(test_list[:]))
+
+        nc.vector.tensor_copy(out=cond_col[:], in_=cond_turned[:, 0:CHUNKS])
 
         w1_code = sb("w1_code", [P, H], U32)
         w1_scale = sb("w1_scale", [P, H], U8)

from contextlib import ExitStack

import concourse.mybir as mybir
from concourse.masks import make_identity

F32 = mybir.dt.float32
BF16 = mybir.dt.bfloat16
I32 = mybir.dt.int32
U32 = mybir.dt.uint32
U16 = mybir.dt.uint16
U8 = mybir.dt.uint8
FP8X4 = mybir.dt.float8_e4m3fn_x4
ACT = mybir.ActivationFunctionType
ALU = mybir.AluOpType

P = 128
PACK = 4
K, T, S, H, N = 512, 2048, 512, 512, 128
HALF = S // 2
CHUNKS = S // P
PC_ON_SCALAR = 2
FLOPS = 2 * K * H * S * 2 + 2 * H * N * S


def tile_picked_yplda_len_p_kernel(tc, x_words, x_scales, w1, e_words, e_scales, cond, across, within, unit, wo, offs, test, out):
    nc = tc.nc
    with ExitStack() as ctx:
        keep = ctx.enter_context(tc.tile_pool(name="keep", bufs=1))
        psum = ctx.enter_context(tc.psum_pool(name="psum", bufs=1))

        def sb(name, shape, dtype, slot=None):
            return keep.tile(shape, dtype, name=name, tag=slot or name, align_bytes=64)

        def dealt(bank):
            return bank[:].rearrange("p (m t) -> p t m", t=PACK)

        def woven(tile_out, tile_in):
            return tile_out.rearrange("p (c i) j -> p c j i", i=4), tile_in.rearrange("p j (c i) -> p c j i", i=4)

        test_list = keep.tile([P, S // 16], U16, name="test_list")
        offs_list = keep.tile([P, S // 16], U16, name="offs_list")
        e_scale_table = sb("e_scale_table", [P, T], U8)
        x_scale_table = sb("x_scale_table", [P, T], U8)
        cond_rows = sb("cond_rows", [P, P], F32)
        nc.vector.memset(cond_rows[:], 0.0)
        nc.gpsimd.memset(e_scale_table[:].bitcast(I32), 0)
        nc.vector.memset(x_scale_table[:].bitcast(I32), 0)
        warm = sb("warm", [P, 2], F32)
        nc.vector.memset(warm[:, 0:1], 1.0)
        nc.scalar.activation(out=warm[:, 1:2], in_=warm[:, 0:1], func=ACT.Abs_reciprocal_sqrt)
        ident = sb("ident", [P, P], F32)
        make_identity(nc, ident[:])

        def load_scales(table, scales):
            for q in range(4):
                nc.sync.dma_start(out=table[32 * q : 32 * q + 4, :].bitcast(I32), in_=scales[0, 4 * q : 4 * q + 4, :].bitcast(I32))

        def load_words(name, words):
            table = sb(name, [P, T], I32)
            nc.sync.dma_start(out=table[:], in_=words[0].rearrange("p n t -> p (n t)").bitcast(I32))
            return table

        def load_column(name, vec):
            col = sb(name, [P, PACK], F32)
            nc.sync.dma_start(out=col[:], in_=vec.rearrange("(p t) o -> p (t o)", t=PACK))
            return col

        nc.sync.dma_start(test_list[:], test)
        w1_rows = w1.rearrange("(p j) c -> p j c", j=PACK)
        w1_raw = []
        for h in range(2):
            raw = sb("w1_raw%d" % h, [P, PACK, H // 2], F32)
            nc.sync.dma_start(out=raw[:], in_=w1_rows[:, :, h * (H // 2) : (h + 1) * (H // 2)])
            w1_raw.append(raw)
        nc.sync.dma_start(out=cond_rows[0:CHUNKS, :], in_=cond[0].rearrange("(g p) -> g p", p=P))
        load_scales(e_scale_table, e_scales)
        e_word_table = load_words("e_word_table", e_words)
        nc.sync.dma_start(offs_list[:], offs)
        load_scales(x_scale_table, x_scales)
        x_word_table = load_words("x_word_table", x_words)
        across_col = load_column("across_col", across)
        within_col = load_column("within_col", within)
        unit_col = load_column("unit_col", unit)
        wo_raw = sb("wo_raw", [P, PACK, N], F32)
        nc.sync.dma_start(out=wo_raw[:], in_=wo.rearrange("(p j) n -> p j n", j=PACK))

        cond_turned = psum.tile([P, P], F32, name="cond_turned", tag="x3")
        nc.tensor.transpose(out=cond_turned[:], in_=cond_rows[:], identity=ident[:])
        cond_col = sb("cond_col", [P, CHUNKS], F32)

        e_scale = sb("e_scale", [P, S], U8)
        nc.vector.tensor_copy(e_scale[:], e_scale_table[:].indirect(test_list[:]))

        nc.vector.tensor_copy(out=cond_col[:], in_=cond_turned[:, 0:CHUNKS])

        w1_code = sb("w1_code", [P, H], U32)
        w1_scale = sb("w1_scale", [P, H], U8)
        for h in range(2):
            part = slice(h * (H // 2), (h + 1) * (H // 2))
            w1_bf = sb("w1_bf%d" % h, [P, H // 2, PACK], BF16)
            dst, src = woven(w1_bf[:], w1_raw[h][:])
            nc.scalar.copy(out=dst, in_=src)
            nc.vector.quantize_mx(out=w1_code[:, part].bitcast(FP8X4), scales=w1_scale[:, part], in_=w1_bf[:].rearrange("p c j -> p (c j)"))

        def project(side, word_table, lst, scale):
            banks = []
            for h in range(2):
                code = sb("%s_code%d" % (side, h), [P, HALF], U32)
                nc.vector.tensor_copy(code[:], word_table[:].bitcast(U32).indirect(lst[:, 16 * h : 16 * h + 16]))
                for u in range(2):
                    g = 2 * h + u
                    bank = psum.tile([P, H], F32, name="%s_bank%d" % (side, g), tag="%s%d" % (side, g))
                    nc.tensor.matmul_mx(
                        out=bank[:],
                        lhsT=code[:, u * P : (u + 1) * P].bitcast(FP8X4),
                        lhsT_scale=scale[:, g * P : (g + 1) * P],
                        rhs=w1_code[:].bitcast(FP8X4),
                        rhs_scale=w1_scale[:],
                        start=True,
                        stop=True,
                    )
                    banks.append(bank)
            return banks

        ebanks = project("e", e_word_table, test_list, e_scale)
        x_scale = sb("x_scale", [P, S], U8, slot="e_word_table")
        nc.vector.tensor_copy(x_scale[:], x_scale_table[:].indirect(offs_list[:]))
        xbanks = project("x", x_word_table, offs_list, x_scale)

        late = sb("late", [P, T], F32, slot="x_word_table")
        cross_w = late[:, 0:PACK]
        square_w = late[:, PACK : 2 * PACK]
        wo_bf = late[:, 16 : 16 + N * PACK // 2].bitcast(BF16)
        wo_code = sb("wo_code", [P, N], U32)
        wo_scale = sb("wo_scale", [P, N], U8)
        pc, sums, crosses, weighted, rinv, qd, zz = {}, {}, {}, {}, {}, {}, {}

        c2 = {}

        def test_scaled(g):
            if g == 0:
                pc[g] = sb("pc0", [P, H], F32)[:].rearrange("p (t m) -> p t m", t=PACK)
            else:
                pc[g] = late[:, g * H : (g + 1) * H].rearrange("p (t m) -> p t m", t=PACK)
            factor = cond_col[:, g : g + 1]
            if g < PC_ON_SCALAR:
                nc.scalar.activation(out=pc[g], in_=dealt(ebanks[g]), func=ACT.Copy, scale=factor)
            else:
                nc.vector.tensor_scalar(out=pc[g], in0=dealt(ebanks[g]), scalar1=factor, scalar2=None, op0=ALU.mult)

        def test_square(g):
            c2[g] = sb("c2%d" % g, [P, PACK, P], F32)
            nc.scalar.activation(out=c2[g][:], in_=dealt(ebanks[g]), func=ACT.Square, scale=cond_col[:, g : g + 1])

        def turn_test(g):
            sums[g] = psum.tile([P, PACK, P], F32, name="sum%d" % g, tag="e%d" % g)
            for t in range(PACK):
                nc.tensor.matmul(out=sums[g][:, t, :], lhsT=c2[g][:, t, :], rhs=ident[:], is_transpose=True, start=(t == 0), stop=False)

        def enrol_square(g):
            a2 = sb("a2%d" % g, [P, PACK, P], F32)
            nc.scalar.activation(out=a2[:], in_=dealt(xbanks[g]), func=ACT.Square)
            for t in range(PACK):
                nc.tensor.matmul(out=sums[g][:, t, :], lhsT=a2[:, t, :], rhs=ident[:], is_transpose=True, start=False, stop=(t == PACK - 1))

        def enrol_product(g):
            prod = sb("prod%d" % g, [P, PACK, P], F32)
            nc.vector.tensor_tensor(out=prod[:], in0=dealt(xbanks[g]), in1=pc[g], op=ALU.mult)
            crosses[g] = psum.tile([P, PACK, P], F32, name="cross%d" % g, tag="x%d" % g)
            for t in range(PACK):
                nc.tensor.transpose(out=crosses[g][:, t, :], in_=prod[:, t, :], identity=ident[:])

        def small_operands():
            nc.vector.tensor_tensor(out=cross_w, in0=across_col[:], in1=unit_col[:], op=ALU.mult)
            nc.vector.scalar_tensor_tensor(out=square_w, in0=within_col[:], scalar=-0.5, in1=unit_col[:], op0=ALU.mult, op1=ALU.mult)
            dst, src = woven(wo_bf.rearrange("p (n j) -> p n j", j=PACK), wo_raw[:])
            nc.vector.tensor_copy(out=dst, in_=src)
            nc.vector.quantize_mx(out=wo_code[:].bitcast(FP8X4), scales=wo_scale[:], in_=wo_bf)

        def combine(g):
            weighted[g] = sb("weighted%d" % g, [P, PACK, P], F32)
            rinv[g] = sb("rinv%d" % g, [P, PACK, P], F32)
            qd[g] = sb("qd%d" % g, [P, PACK, P], F32)
            root_first = g == CHUNKS - 1
            if root_first:
                nc.scalar.activation(out=rinv[g][:], in_=sums[g][:], func=ACT.Abs_reciprocal_sqrt, bias=0.3)
            for t in range(PACK):
                nc.scalar.activation(out=weighted[g][:, t, :], in_=sums[g][:, t, :], func=ACT.Copy, scale=square_w[:, t : t + 1])
            if not root_first:
                nc.scalar.activation(out=rinv[g][:], in_=sums[g][:], func=ACT.Abs_reciprocal_sqrt, bias=0.3)
            for t in range(PACK):
                nc.vector.scalar_tensor_tensor(out=qd[g][:, t, :], in0=crosses[g][:, t, :], scalar=cross_w[:, t : t + 1], in1=weighted[g][:, t, :], op0=ALU.mult, op1=ALU.add)

        def score(g, target):
            zz = sb("zz%d" % g, [P, P, PACK], BF16)
            nc.vector.tensor_tensor(
                out=zz[:].rearrange("p (c i) t -> p c t i", i=4),
                in0=qd[g][:].rearrange("p t (c i) -> p c t i", i=4),
                in1=rinv[g][:].rearrange("p t (c i) -> p c t i", i=4),
                op=ALU.mult,
            )
            zz_code = sb("zz_code%d" % g, [P, P], U32)
            zz_scale = sb("zz_scale%d" % g, [P, P], U8)
            nc.vector.quantize_mx(out=zz_code[:].bitcast(FP8X4), scales=zz_scale[:], in_=zz[:].rearrange("p c t -> p (c t)"))
            nc.tensor.matmul_mx(
                out=target,
                lhsT=wo_code[:].bitcast(FP8X4),
                lhsT_scale=wo_scale[:],
                rhs=zz_code[:].bitcast(FP8X4),
                rhs_scale=zz_scale[:],
                start=True,
                stop=True,
            )

        last = CHUNKS - 1
        test_scaled(0)
        test_square(0)
        turn_test(0)
        test_square(1)
        enrol_square(0)
        test_scaled(1)
        turn_test(1)
        enrol_product(0)
        small_operands()
        scores = []
        for g in range(CHUNKS):
            if g + 2 < CHUNKS:
                test_scaled(g + 2)
            if g + 1 < CHUNKS:
                enrol_square(g + 1)
                enrol_product(g + 1)
            if g + 2 < CHUNKS:
                test_square(g + 2)
                turn_test(g + 2)
            combine(g)
            scores.append(psum.tile([P, P], F32, name="scores%d" % g, tag="e%d" % g))
            score(g, scores[g][:])
        res = weighted[last]
        for g in range(CHUNKS):
            nc.scalar.activation(out=res[:, g, :], in_=scores[g][:], func=ACT.Tanh)
            if g >= last - 1:
                first = 0 if g < last else last
                nc.sync.dma_start(out=out[:, first * P : (g + 1) * P], in_=res[:, first : g + 1, :].rearrange("p g c -> p (g c)"))
